import numpy as np
import ml_dtypes


def mxq(x, axis, fmt="e4m3"):
    dtype, down = {"e4m3": (ml_dtypes.float8_e4m3fn, 7), "e5m2": (ml_dtypes.float8_e5m2, 14)}[fmt]
    v = np.moveaxis(np.asarray(x, np.float32).astype(ml_dtypes.bfloat16).astype(np.float64), axis, -1)
    blocks = v.reshape(v.shape[:-1] + (-1, 32))
    amax = np.abs(blocks).max(-1, keepdims=True)
    byte = np.maximum(np.where(amax > 0, np.frexp(amax)[1] - 1 + 127, 0) - down, 1)
    scale = np.exp2(byte - 127.0)
    codes = (blocks / scale).astype(np.float32).astype(dtype).astype(np.float64)
    return np.moveaxis((codes * scale).reshape(v.shape), -1, axis)


WIDE = False


def mx_kscale(k):
    if not WIDE:
        return np.ones(k)
    levels = np.array([30, -30])
    if k % 512:
        return np.exp2(np.random.permutation(np.resize(levels, k // 32))).repeat(32)
    a = np.empty((k // 512, 16))
    for p in range(k // 512):
        a[p, :8] = np.random.permutation(np.resize(levels, 8))
        for g in range(8):
            far = levels[np.abs(levels - a[p, g]) >= 10]
            a[p, g + 8] = far[np.random.randint(len(far))]
    return np.exp2(a.ravel()).repeat(32)


def f64(x):
    return np.asarray(x).astype(np.float64)


def striped(idx):
    return np.tile(np.asarray(idx).reshape(-1, 16).T, (8, 1)).astype(np.uint16)


def unstriped(offs):
    return offs[:16].T.reshape(-1).astype(np.int64)


E2M1 = np.array([0.0, 0.5, 1.0, 1.5, 2.0, 3.0, 4.0, 6.0, -0.0, -0.5, -1.0, -1.5, -2.0, -3.0, -4.0, -6.0])


def pack_weight(w, fmt):
    k, n = w.shape
    w = f64(np.asarray(w, np.float32).astype(ml_dtypes.bfloat16)).reshape(k // 32, 32, n)
    amax = np.abs(w).max(1)
    if fmt == "e4m3":
        byte = np.frexp(amax)[1] - 1 + 127 - 7
    else:
        mant, ex = np.frexp(amax / 6.0)
        byte = np.where(mant > 0.5, ex, ex - 1) + 127
    byte = np.clip(np.where(amax > 0, byte, 1), 1, 254)
    scaled = (w * np.exp2(127.0 - byte)[:, None, :]).reshape(k, n).astype(np.float32)
    by_word = np.ascontiguousarray(scaled.reshape(k // 512, 128, 4, n).transpose(0, 1, 3, 2))
    if fmt == "e4m3":
        words = by_word.astype(ml_dtypes.float8_e4m3fn).view(np.uint8)
    else:
        c = by_word.astype(ml_dtypes.float4_e2m1fn).view(np.uint8) & 0xF
        words = (c[..., 0::2] | (c[..., 1::2] << 4)).reshape(k // 512, 128, 2 * n)
    return np.ascontiguousarray(words), np.ascontiguousarray(byte.astype(np.uint8).reshape(k // 512, 16, n))


def unpack_weight(words, scales, fmt):
    g, _, n = scales.shape
    words = np.ascontiguousarray(words).reshape(g, 128, n, -1)
    if fmt == "e4m3":
        vals = words.view(ml_dtypes.float8_e4m3fn).astype(np.float64)
    else:
        nib = np.empty((g, 128, n, 4), np.uint8)
        nib[..., 0::2] = words & 0xF
        nib[..., 1::2] = words >> 4
        vals = E2M1[nib]
    vals = vals * np.repeat(np.exp2(scales.astype(np.float64) - 127.0), 8, axis=1)[..., None]
    return vals.transpose(0, 1, 3, 2).reshape(g * 512, n)


def bf(x):
    return np.asarray(x, np.float32).astype(ml_dtypes.bfloat16)


def planes(Y):
    r, m = Y.shape
    b = f64(bf(Y)).reshape(r // 32, 32, m)
    amax = np.abs(b).max(1)
    byte = np.clip(np.where(amax > 0, np.frexp(amax)[1] - 1 + 127 - 7, 1), 1, 254)
    codes = (b * np.exp2(127.0 - byte)[:, None, :]).reshape(r, m).astype(np.float32).astype(ml_dtypes.float8_e4m3fn).view(np.uint8)
    words = codes.reshape(r // 512, 128, 4, m).transpose(0, 1, 3, 2)
    return np.ascontiguousarray(words), np.ascontiguousarray(byte.astype(np.uint8).reshape(r // 512, 16, m))


K, N, T, J = 512, 512, 1024, 512


def setup_inputs():
    n = np.random.standard_normal
    idx = np.random.permutation(T)[:J]
    fk = mx_kscale(K)
    fn = mx_kscale(N)
    xtp = pack_weight(n((K, T)) / fk[:, None], "e2m1")
    wap = pack_weight(n((K, N)) * 1 / np.sqrt(K) * fk[:, None], "e4m3")
    wbp = pack_weight(n((K, N)) * 1 / np.sqrt(K) * fk[:, None], "e2m1")
    wtp = pack_weight(n((N, K)) * 1 / np.sqrt(N) / fn[:, None], "e4m3")
    return {
        "xt_words": xtp[0],
        "xt_scales": xtp[1],
        "wa_words": wap[0],
        "wa_scales": wap[1],
        "wb_words": wbp[0],
        "wb_scales": wbp[1],
        "us": (np.random.uniform(0.5, 2.0, (N, 1)) * fn[:, None]).astype(np.float32),
        "wt_words": wtp[0],
        "wt_scales": wtp[1],
        "rw": (np.random.uniform(0.5, 2.0, (1, J))).astype(np.float32),
        "offs": striped(idx),
    }


def reference(xt_words, xt_scales, wa_words, wa_scales, wb_words, wb_scales, us, wt_words, wt_scales, rw, offs):
    idx = unstriped(offs)
    xtu = unpack_weight(xt_words, xt_scales, "e2m1")
    wau = unpack_weight(wa_words, wa_scales, "e4m3")
    wbu = unpack_weight(wb_words, wb_scales, "e2m1")
    wtu = unpack_weight(wt_words, wt_scales, "e4m3")
    xtidxg = xtu[:, idx]
    a = wau.T @ xtidxg
    b = wbu.T @ xtidxg
    d = np.tanh(a - b) * f64(us)
    dq = mxq(d, 0, "e5m2")
    q = wtu.T @ dq
    y = q * f64(rw)
    words, scales = planes(y)
    return y, words, scales

@@ -1,0 +1,193 @@
+from contextlib import ExitStack
+
+import concourse.mybir as mybir
+from concourse.masks import make_identity
+
+K, N, T, J = 512, 512, 1024, 512
+FLOPS = 3 * 2 * K * N * J
+
+F32 = mybir.dt.float32
+BF16 = mybir.dt.bfloat16
+I32 = mybir.dt.int32
+U32 = mybir.dt.uint32
+U16 = mybir.dt.uint16
+U8 = mybir.dt.uint8
+E4M3 = mybir.dt.float8_e4m3fn_x4
+E5M2 = mybir.dt.float8_e5m2_x4
+E2M1 = mybir.dt.float4_e2m1fn_x4
+ACT = mybir.ActivationFunctionType
+ALU = mybir.AluOpType
+
+P = 128
+PACK = 4
+CHUNKS = J // P
+HALVES = 2
+HALF = J // HALVES
+
+
+def load_scales(queues, plane, rows, quads=range(4)):
+    width = rows.shape[2] // 4
+    src = rows[0].bitcast(I32)
+    for q in quads:
+        block = src[4 * q : 4 * q + 4, :].rearrange("(o r) w -> o r w", o=1).to_broadcast([8, 4, width])
+        queues[q % len(queues)].dma_start(out=plane[32 * q : 32 * q + 32, :].bitcast(I32), in_=block)
+
+
+def tile_moe_experts_pulled_together_pl_kernel(
+    tc, xt_words, xt_scales, wa_words, wa_scales, wb_words, wb_scales, us, wt_words, wt_scales, rw, offs,
+    out_0, out_1, out_2,
+):
+    nc = tc.nc
+    with ExitStack() as ctx:
+        held = ctx.enter_context(tc.tile_pool(name="held", bufs=1))
+        work = ctx.enter_context(tc.tile_pool(name="work", bufs=CHUNKS))
+        psum = ctx.enter_context(tc.psum_pool(name="psum", bufs=8))
+        both = [nc.sync, nc.scalar]
+
+        offsets = held.tile([P, J // 16], U16, name="offsets")
+        xw = held.tile([P, 2 * T], U8, name="xw", align_bytes=64)
+        xs = held.tile([P, T], U8, name="xs", align_bytes=64)
+        wa = held.tile([P, 4 * N], U8, name="wa", align_bytes=64)
+        was = held.tile([P, N], U8, name="was", align_bytes=64)
+        wb = held.tile([P, 2 * N], U8, name="wb", align_bytes=64)
+        wbs = held.tile([P, N], U8, name="wbs", align_bytes=64)
+        wt = held.tile([P, 4 * K], U8, name="wt", align_bytes=64)
+        wts = held.tile([P, K], U8, name="wts", align_bytes=64)
+        us_sb = held.tile([P, 1, PACK], F32, name="us_sb")
+        rw_sb = held.tile([P, CHUNKS], F32, name="rw_sb")
+        ident = held.tile([P, P], F32, name="ident")
+        warm = held.tile([P, 8], F32, name="warm")
+        warm_out = held.tile([P, 8], F32, name="warm_out")
+        y_codes = held.tile([P, J], U32, name="y_codes", align_bytes=64)
+        y_scales = held.tile([P, J], U8, name="y_scales", align_bytes=64)
+
+        nc.sync.dma_start(offsets[:], offs)
+        nc.scalar.dma_start(out=xw[:].bitcast(I32), in_=xt_words[0].bitcast(I32))
+        load_scales(both, xs, xt_scales)
+        load_scales(both, wbs, wb_scales, range(0, 2))
+        nc.vector.memset(warm[:], 0.0)
+        nc.scalar.activation(out=warm_out[:], in_=warm[:], func=ACT.Tanh)
+        nc.sync.dma_start(out=wb[:].bitcast(I32), in_=wb_words[0].bitcast(I32))
+        nc.sync.dma_start(out=wa[:].bitcast(I32), in_=wa_words[0].rearrange("p n t -> p (n t)").bitcast(I32))
+        load_scales([nc.sync], wbs, wb_scales, range(2, 4))
+        load_scales([nc.sync], was, wa_scales)
+        nc.sync.dma_start(out=us_sb[:], in_=us.rearrange("(p t) o -> p o t", t=PACK))
+        nc.sync.dma_start(out=wt[:].bitcast(I32), in_=wt_words[0].rearrange("p n t -> p (n t)").bitcast(I32))
+        load_scales([nc.sync], wts, wt_scales)
+        with nc.allow_non_contiguous_dma(reason="one weight a partition"):
+            nc.sync.dma_start(out=rw_sb[:], in_=rw.rearrange("o (c p) -> p (o c)", p=P))
+        make_identity(nc, ident[:])
+
+        for i in range(3):
+            bank = psum.tile([P, N], F32, name="bank", tag="bank")
+            nc.tensor.matmul_mx(
+                out=bank[:], lhsT=xw[:, 0 : 2 * P].bitcast(E2M1), lhsT_scale=xs[:, 0:P],
+                rhs=xw[:, 0 : 2 * N].bitcast(E2M1), rhs_scale=xs[:, 0:N], start=True, stop=True,
+            )
+
+        gw, gs = [], []
+        for h in range(HALVES):
+            cols = slice(h * HALF // 16, (h + 1) * HALF // 16)
+            words = held.tile([P, 2 * HALF], U8, name="gw%d" % h, align_bytes=64)
+            scales = held.tile([P, HALF], U8, name="gs%d" % h, align_bytes=64)
+            nc.vector.tensor_copy(words[:].bitcast(U16), xw[:].bitcast(U16).indirect(offsets[:, cols]))
+            nc.vector.tensor_copy(scales[:], xs[:].indirect(offsets[:, cols]))
+            gw.append(words)
+            gs.append(scales)
+
+        st = [dict() for c in range(CHUNKS)]
+        out_view = out_0.rearrange("(p t) j -> p t j", t=PACK)
+        words_view = out_1[0].rearrange("p c t -> p (c t)").bitcast(I32)
+
+        def products(c):
+            h, o = divmod(c * P, HALF)
+            for key, w, ws, fmt in (("b", wb, wbs, E2M1), ("a", wa, was, E4M3)):
+                bank = psum.tile([P, N], F32, name="bank", tag="bank")
+                nc.tensor.matmul_mx(
+                    out=bank[:],
+                    lhsT=gw[h][:, 2 * o : 2 * (o + P)].bitcast(E2M1), lhsT_scale=gs[h][:, o : o + P],
+                    rhs=w[:].bitcast(fmt), rhs_scale=ws[:], start=True, stop=True,
+                )
+                st[c][key] = bank
+
+        def copy_b(c):
+            b_sb = work.tile([P, PACK, P], F32, name="b_sb")
+            nc.scalar.copy(out=b_sb[:], in_=st[c]["b"][:].rearrange("p (m t) -> p t m", t=PACK))
+            st[c]["b_sb"] = b_sb
+
+        def gap(c):
+            z = work.tile([P, PACK, P], F32, name="z")
+            nc.vector.tensor_tensor(z[:], st[c]["a"][:].rearrange("p (m t) -> p t m", t=PACK), st[c]["b_sb"][:], ALU.subtract)
+            st[c]["z"] = z
+
+        def squash(c):
+            th = work.tile([P, PACK, P], F32, name="th")
+            nc.scalar.activation(out=th[:], in_=st[c]["z"][:], func=ACT.Tanh)
+            st[c]["th"] = th
+
+        def turn(c, src, dst):
+            bank = psum.tile([P, PACK, P], F32, name="bank", tag="bank")
+            for t in range(PACK):
+                nc.tensor.transpose(bank[:, t, :], st[c][src][:, t, :], ident[:])
+            st[c][dst] = bank
+
+        def weigh(c):
+            d = work.tile([P, P, PACK], BF16, name="d", align_bytes=64)
+            nc.vector.tensor_tensor(
+                d[:], st[c]["th_t"][:].rearrange("p t j -> p j t"), us_sb[:].to_broadcast([P, P, PACK]), ALU.mult
+            )
+            st[c]["d"] = d
+
+        def quantise_d(c):
+            codes = work.tile([P, P], U32, name="d_codes", align_bytes=64)
+            scales = work.tile([P, P], U8, name="d_scales", align_bytes=64)
+            nc.vector.quantize_mx(out=codes[:].bitcast(E5M2), scales=scales[:], in_=st[c]["d"][:].rearrange("p j t -> p (j t)"))
+            st[c]["dq"] = (codes, scales)
+
+        def way_back(c):
+            codes, scales = st[c]["dq"]
+            bank = psum.tile([P, K], F32, name="bank", tag="bank")
+            nc.tensor.matmul_mx(
+                out=bank[:], lhsT=codes[:].bitcast(E5M2), lhsT_scale=scales[:],
+                rhs=wt[:].bitcast(E4M3), rhs_scale=wts[:], start=True, stop=True,
+            )
+            st[c]["q"] = bank
+
+        def scale_rows(c):
+            y_t = work.tile([P, PACK, P], F32, name="y_t")
+            nc.scalar.activation(
+                out=y_t[:], in_=st[c]["q"][:].rearrange("p (m t) -> p t m", t=PACK), func=ACT.Copy, scale=rw_sb[:, c : c + 1]
+            )
+            st[c]["y_t"] = y_t
+
+        def round_y(c):
+            y_bf = work.tile([P, P, PACK], BF16, name="y_bf", align_bytes=64)
+            nc.vector.tensor_copy(y_bf[:], st[c]["y"][:].rearrange("p t j -> p j t"))
+            st[c]["y_bf"] = y_bf
+
+        def store_y(c):
+            y_sb = work.tile([P, PACK, P], F32, name="y_sb")
+            nc.scalar.copy(out=y_sb[:], in_=st[c]["y"][:])
+            nc.sync.dma_start(out=out_view[:, :, c * P : (c + 1) * P], in_=y_sb[:])
+
+        def quantise_y(c):
+            cols = slice(c * P, (c + 1) * P)
+            nc.vector.quantize_mx(
+                out=y_codes[:, cols].bitcast(E4M3), scales=y_scales[:, cols], in_=st[c]["y_bf"][:].rearrange("p j t -> p (j t)")
+            )
+            nc.sync.dma_start(out=words_view[:, cols], in_=y_codes[:, cols].bitcast(I32))
+
+        stages = [
+            products, copy_b, gap, squash, lambda c: turn(c, "th", "th_t"), weigh, quantise_d, way_back,
+            scale_rows, lambda c: turn(c, "y_t", "y"), round_y, store_y, quantise_y,
+        ]
+        LAG = 1
+        for step in range(len(stages) + LAG * (CHUNKS - 1)):
+            for c in range(CHUNKS):
+                s = step - LAG * c
+                if 0 <= s < len(stages):
+                    stages[s](c)
+
+        scales_view = out_2[0].bitcast(I32)
+        for q in range(4):
+            both[q % 2].dma_start(out=scales_view[4 * q : 4 * q + 4, :], in_=y_scales[32 * q : 32 * q + 4, :].bitcast(I32))

@@ -25,12 +25,10 @@ HALVES = 2
 HALF = J // HALVES
 
 
-def load_scales(queues, plane, rows, quads=range(4)):
-    width = rows.shape[2] // 4
+def load_scales(nc, plane, rows):
     src = rows[0].bitcast(I32)
-    for q in quads:
-        block = src[4 * q : 4 * q + 4, :].rearrange("(o r) w -> o r w", o=1).to_broadcast([8, 4, width])
-        queues[q % len(queues)].dma_start(out=plane[32 * q : 32 * q + 32, :].bitcast(I32), in_=block)
+    for q in range(4):
+        nc.sync.dma_start(out=plane[32 * q : 32 * q + 4, :].bitcast(I32), in_=src[4 * q : 4 * q + 4, :])
 
 
 def tile_moe_experts_pulled_together_pl_kernel(
@@ -39,19 +37,19 @@ def tile_moe_experts_pulled_together_pl_kernel(
 ):
     nc = tc.nc
     with ExitStack() as ctx:
+        lists = ctx.enter_context(tc.tile_pool(name="lists", bufs=1))
         held = ctx.enter_context(tc.tile_pool(name="held", bufs=1))
         work = ctx.enter_context(tc.tile_pool(name="work", bufs=CHUNKS))
         psum = ctx.enter_context(tc.psum_pool(name="psum", bufs=8))
         both = [nc.sync, nc.scalar]
 
-        offsets = held.tile([P, J // 16], U16, name="offsets")
-        xw = held.tile([P, 2 * T], U8, name="xw", align_bytes=64)
+        offsets = lists.tile([P, J // 16], U16, name="offsets")
+        xw = held.tile([P, 2 * T], U8, name="xw", tag="words", align_bytes=64)
         xs = held.tile([P, T], U8, name="xs", align_bytes=64)
         wa = held.tile([P, 4 * N], U8, name="wa", align_bytes=64)
         was = held.tile([P, N], U8, name="was", align_bytes=64)
         wb = held.tile([P, 2 * N], U8, name="wb", align_bytes=64)
         wbs = held.tile([P, N], U8, name="wbs", align_bytes=64)
-        wt = held.tile([P, 4 * K], U8, name="wt", align_bytes=64)
         wts = held.tile([P, K], U8, name="wts", align_bytes=64)
         us_sb = held.tile([P, 1, PACK], F32, name="us_sb")
         rw_sb = held.tile([P, CHUNKS], F32, name="rw_sb")
@@ -61,22 +59,22 @@ def tile_moe_experts_pulled_together_pl_kernel(
         y_codes = held.tile([P, J], U32, name="y_codes", align_bytes=64)
         y_scales = held.tile([P, J], U8, name="y_scales", align_bytes=64)
 
+        for plane in (xs, wbs, was, wts):
+            nc.vector.memset(plane[:].bitcast(I32), 0)
         nc.sync.dma_start(offsets[:], offs)
         nc.scalar.dma_start(out=xw[:].bitcast(I32), in_=xt_words[0].bitcast(I32))
-        load_scales(both, xs, xt_scales)
-        load_scales(both, wbs, wb_scales, range(0, 2))
+        nc.scalar.dma_start(out=wb[:].bitcast(I32), in_=wb_words[0].bitcast(I32))
+        nc.scalar.dma_start(out=wa[:].bitcast(I32), in_=wa_words[0].rearrange("p n t -> p (n t)").bitcast(I32))
+        load_scales(nc, xs, xt_scales)
         nc.vector.memset(warm[:], 0.0)
         nc.scalar.activation(out=warm_out[:], in_=warm[:], func=ACT.Tanh)
-        nc.sync.dma_start(out=wb[:].bitcast(I32), in_=wb_words[0].bitcast(I32))
-        nc.sync.dma_start(out=wa[:].bitcast(I32), in_=wa_words[0].rearrange("p n t -> p (n t)").bitcast(I32))
-        load_scales([nc.sync], wbs, wb_scales, range(2, 4))
-        load_scales([nc.sync], was, wa_scales)
-        nc.sync.dma_start(out=us_sb[:], in_=us.rearrange("(p t) o -> p o t", t=PACK))
-        nc.sync.dma_start(out=wt[:].bitcast(I32), in_=wt_words[0].rearrange("p n t -> p (n t)").bitcast(I32))
-        load_scales([nc.sync], wts, wt_scales)
-        with nc.allow_non_contiguous_dma(reason="one weight a partition"):
-            nc.sync.dma_start(out=rw_sb[:], in_=rw.rearrange("o (c p) -> p (o c)", p=P))
+        load_scales(nc, wbs, wb_scales)
+        load_scales(nc, was, wa_scales)
+        load_scales(nc, wts, wt_scales)
         make_identity(nc, ident[:])
+        nc.gpsimd.dma_start(out=us_sb[:], in_=us.rearrange("(p t) o -> p o t", t=PACK))
+        with nc.allow_non_contiguous_dma(reason="one weight a partition"):
+            nc.gpsimd.dma_start(out=rw_sb[:], in_=rw.rearrange("o (c p) -> p (o c)", p=P))
 
         for i in range(3):
             bank = psum.tile([P, N], F32, name="bank", tag="bank")
@@ -95,24 +93,33 @@ def tile_moe_experts_pulled_together_pl_kernel(
             gw.append(words)
             gs.append(scales)
 
+        wt = held.tile([P, 4 * K], U8, name="wt", tag="words", align_bytes=64)
+        nc.sync.dma_start(out=wt[:].bitcast(I32), in_=wt_words[0].rearrange("p n t -> p (n t)").bitcast(I32))
+
         st = [dict() for c in range(CHUNKS)]
         out_view = out_0.rearrange("(p t) j -> p t j", t=PACK)
         words_view = out_1[0].rearrange("p c t -> p (c t)").bitcast(I32)
 
-        def products(c):
+        def product(c, key, w, ws, fmt):
             h, o = divmod(c * P, HALF)
-            for key, w, ws, fmt in (("b", wb, wbs, E2M1), ("a", wa, was, E4M3)):
-                bank = psum.tile([P, N], F32, name="bank", tag="bank")
-                nc.tensor.matmul_mx(
-                    out=bank[:],
-                    lhsT=gw[h][:, 2 * o : 2 * (o + P)].bitcast(E2M1), lhsT_scale=gs[h][:, o : o + P],
-                    rhs=w[:].bitcast(fmt), rhs_scale=ws[:], start=True, stop=True,
-                )
-                st[c][key] = bank
+            bank = psum.tile([P, N], F32, name="bank", tag="bank")
+            nc.tensor.matmul_mx(
+                out=bank[:],
+                lhsT=gw[h][:, 2 * o : 2 * (o + P)].bitcast(E2M1), lhsT_scale=gs[h][:, o : o + P],
+                rhs=w[:].bitcast(fmt), rhs_scale=ws[:], start=True, stop=True,
+            )
+            st[c][key] = bank
+
+        def pieces(c):
+            return [slice(0, 2), slice(2, 4)] if c == CHUNKS - 1 else [slice(0, 4)]
 
         def copy_b(c):
             b_sb = work.tile([P, PACK, P], F32, name="b_sb")
-            nc.scalar.copy(out=b_sb[:], in_=st[c]["b"][:].rearrange("p (m t) -> p t m", t=PACK))
+            src = st[c]["b"][:].rearrange("p (m t) -> p t m", t=PACK)
+            if c == 1:
+                nc.vector.tensor_copy(b_sb[:], src)
+            else:
+                nc.scalar.copy(out=b_sb[:], in_=src)
             st[c]["b_sb"] = b_sb
 
         def gap(c):
@@ -122,7 +129,8 @@ def tile_moe_experts_pulled_together_pl_kernel(
 
         def squash(c):
             th = work.tile([P, PACK, P], F32, name="th")
-            nc.scalar.activation(out=th[:], in_=st[c]["z"][:], func=ACT.Tanh)
+            for ts in pieces(c):
+                nc.scalar.activation(out=th[:, ts, :], in_=st[c]["z"][:, ts, :], func=ACT.Tanh)
             st[c]["th"] = th
 
         def turn(c, src, dst):
@@ -155,38 +163,54 @@ def tile_moe_experts_pulled_together_pl_kernel(
 
         def scale_rows(c):
             y_t = work.tile([P, PACK, P], F32, name="y_t")
-            nc.scalar.activation(
-                out=y_t[:], in_=st[c]["q"][:].rearrange("p (m t) -> p t m", t=PACK), func=ACT.Copy, scale=rw_sb[:, c : c + 1]
-            )
+            src = st[c]["q"][:].rearrange("p (m t) -> p t m", t=PACK)
+            for ts in pieces(c):
+                nc.scalar.activation(out=y_t[:, ts, :], in_=src[:, ts, :], func=ACT.Copy, scale=rw_sb[:, c : c + 1])
             st[c]["y_t"] = y_t
 
-        def round_y(c):
+        def copy(on_vector, out, src):
+            if on_vector:
+                nc.vector.tensor_copy(out, src)
+            else:
+                nc.scalar.copy(out=out, in_=src)
+
+        def round_y(c, on_vector, src):
             y_bf = work.tile([P, P, PACK], BF16, name="y_bf", align_bytes=64)
-            nc.vector.tensor_copy(y_bf[:], st[c]["y"][:].rearrange("p t j -> p j t"))
+            copy(on_vector, y_bf[:], src[:].rearrange("p t j -> p j t"))
             st[c]["y_bf"] = y_bf
 
         def store_y(c):
             y_sb = work.tile([P, PACK, P], F32, name="y_sb")
-            nc.scalar.copy(out=y_sb[:], in_=st[c]["y"][:])
+            early = c < 2
+            if not early:
+                round_y(c, c == CHUNKS - 1, st[c]["y"])
+            copy(early, y_sb[:], st[c]["y"][:])
             nc.sync.dma_start(out=out_view[:, :, c * P : (c + 1) * P], in_=y_sb[:])
+            if early:
+                round_y(c, True, y_sb)
 
         def quantise_y(c):
             cols = slice(c * P, (c + 1) * P)
             nc.vector.quantize_mx(
                 out=y_codes[:, cols].bitcast(E4M3), scales=y_scales[:, cols], in_=st[c]["y_bf"][:].rearrange("p j t -> p (j t)")
             )
-            nc.sync.dma_start(out=words_view[:, cols], in_=y_codes[:, cols].bitcast(I32))
+            if c % 2 == 1:
+                pair = slice((c - 1) * P, (c + 1) * P)
+                nc.sync.dma_start(out=words_view[:, pair], in_=y_codes[:, pair].bitcast(I32))
+
+        product(0, "b", wb, wbs, E2M1)
+        for c in range(CHUNKS):
+            if c + 1 < CHUNKS:
+                product(c + 1, "b", wb, wbs, E2M1)
+            product(c, "a", wa, was, E4M3)
 
         stages = [
-            products, copy_b, gap, squash, lambda c: turn(c, "th", "th_t"), weigh, quantise_d, way_back,
-            scale_rows, lambda c: turn(c, "y_t", "y"), round_y, store_y, quantise_y,
+            copy_b, gap, squash, lambda c: turn(c, "th", "th_t"), weigh, quantise_d, way_back,
+            scale_rows, lambda c: turn(c, "y_t", "y"), store_y, quantise_y,
         ]
-        LAG = 1
-        for step in range(len(stages) + LAG * (CHUNKS - 1)):
+        for stage in stages:
             for c in range(CHUNKS):
-                s = step - LAG * c
-                if 0 <= s < len(stages):
-                    stages[s](c)
+                stage(c)
 
         scales_view = out_2[0].bitcast(I32)
         for q in range(4):

from contextlib import ExitStack

import concourse.mybir as mybir
from concourse.masks import make_identity

K, N, T, J = 512, 512, 1024, 512
FLOPS = 3 * 2 * K * N * J

F32 = mybir.dt.float32
BF16 = mybir.dt.bfloat16
I32 = mybir.dt.int32
U32 = mybir.dt.uint32
U16 = mybir.dt.uint16
U8 = mybir.dt.uint8
E4M3 = mybir.dt.float8_e4m3fn_x4
E5M2 = mybir.dt.float8_e5m2_x4
E2M1 = mybir.dt.float4_e2m1fn_x4
ACT = mybir.ActivationFunctionType
ALU = mybir.AluOpType

P = 128
PACK = 4
CHUNKS = J // P
HALVES = 2
HALF = J // HALVES


def load_scales(nc, plane, rows):
    src = rows[0].bitcast(I32)
    for q in range(4):
        nc.sync.dma_start(out=plane[32 * q : 32 * q + 4, :].bitcast(I32), in_=src[4 * q : 4 * q + 4, :])


def tile_moe_experts_pulled_together_pl_kernel(
    tc, xt_words, xt_scales, wa_words, wa_scales, wb_words, wb_scales, us, wt_words, wt_scales, rw, offs,
    out_0, out_1, out_2,
):
    nc = tc.nc
    with ExitStack() as ctx:
        lists = ctx.enter_context(tc.tile_pool(name="lists", bufs=1))
        held = ctx.enter_context(tc.tile_pool(name="held", bufs=1))
        work = ctx.enter_context(tc.tile_pool(name="work", bufs=CHUNKS))
        psum = ctx.enter_context(tc.psum_pool(name="psum", bufs=8))
        both = [nc.sync, nc.scalar]

        offsets = lists.tile([P, J // 16], U16, name="offsets")
        xw = held.tile([P, 2 * T], U8, name="xw", tag="words", align_bytes=64)
        xs = held.tile([P, T], U8, name="xs", align_bytes=64)
        wa = held.tile([P, 4 * N], U8, name="wa", align_bytes=64)
        was = held.tile([P, N], U8, name="was", align_bytes=64)
        wb = held.tile([P, 2 * N], U8, name="wb", align_bytes=64)
        wbs = held.tile([P, N], U8, name="wbs", align_bytes=64)
        wts = held.tile([P, K], U8, name="wts", align_bytes=64)
        us_sb = held.tile([P, 1, PACK], F32, name="us_sb")
        rw_sb = held.tile([P, CHUNKS], F32, name="rw_sb")
        ident = held.tile([P, P], F32, name="ident")
        warm = held.tile([P, 8], F32, name="warm")
        warm_out = held.tile([P, 8], F32, name="warm_out")
        y_codes = held.tile([P, J], U32, name="y_codes", align_bytes=64)
        y_scales = held.tile([P, J], U8, name="y_scales", align_bytes=64)

        for plane in (xs, wbs, was, wts):
            nc.vector.memset(plane[:].bitcast(I32), 0)
        nc.sync.dma_start(offsets[:], offs)
        nc.scalar.dma_start(out=xw[:].bitcast(I32), in_=xt_words[0].bitcast(I32))
        nc.scalar.dma_start(out=wb[:].bitcast(I32), in_=wb_words[0].bitcast(I32))
        nc.scalar.dma_start(out=wa[:].bitcast(I32), in_=wa_words[0].rearrange("p n t -> p (n t)").bitcast(I32))
        load_scales(nc, xs, xt_scales)
        nc.vector.memset(warm[:], 0.0)
        nc.scalar.activation(out=warm_out[:], in_=warm[:], func=ACT.Tanh)
        load_scales(nc, wbs, wb_scales)
        load_scales(nc, was, wa_scales)
        load_scales(nc, wts, wt_scales)
        make_identity(nc, ident[:])
        nc.gpsimd.dma_start(out=us_sb[:], in_=us.rearrange("(p t) o -> p o t", t=PACK))
        with nc.allow_non_contiguous_dma(reason="one weight a partition"):
            nc.gpsimd.dma_start(out=rw_sb[:], in_=rw.rearrange("o (c p) -> p (o c)", p=P))

        for i in range(3):
            bank = psum.tile([P, N], F32, name="bank", tag="bank")
            nc.tensor.matmul_mx(
                out=bank[:], lhsT=xw[:, 0 : 2 * P].bitcast(E2M1), lhsT_scale=xs[:, 0:P],
                rhs=xw[:, 0 : 2 * N].bitcast(E2M1), rhs_scale=xs[:, 0:N], start=True, stop=True,
            )

        gw, gs = [], []
        for h in range(HALVES):
            cols = slice(h * HALF // 16, (h + 1) * HALF // 16)
            words = held.tile([P, 2 * HALF], U8, name="gw%d" % h, align_bytes=64)
            scales = held.tile([P, HALF], U8, name="gs%d" % h, align_bytes=64)
            nc.vector.tensor_copy(words[:].bitcast(U16), xw[:].bitcast(U16).indirect(offsets[:, cols]))
            nc.vector.tensor_copy(scales[:], xs[:].indirect(offsets[:, cols]))
            gw.append(words)
            gs.append(scales)

        wt = held.tile([P, 4 * K], U8, name="wt", tag="words", align_bytes=64)
        nc.sync.dma_start(out=wt[:].bitcast(I32), in_=wt_words[0].rearrange("p n t -> p (n t)").bitcast(I32))

        st = [dict() for c in range(CHUNKS)]
        out_view = out_0.rearrange("(p t) j -> p t j", t=PACK)
        words_view = out_1[0].rearrange("p c t -> p (c t)").bitcast(I32)

        def product(c, key, w, ws, fmt):
            h, o = divmod(c * P, HALF)
            bank = psum.tile([P, N], F32, name="bank", tag="bank")
            nc.tensor.matmul_mx(
                out=bank[:],
                lhsT=gw[h][:, 2 * o : 2 * (o + P)].bitcast(E2M1), lhsT_scale=gs[h][:, o : o + P],
                rhs=w[:].bitcast(fmt), rhs_scale=ws[:], start=True, stop=True,
            )
            st[c][key] = bank

        def pieces(c):
            return [slice(0, 2), slice(2, 4)] if c == CHUNKS - 1 else [slice(0, 4)]

        def copy_b(c):
            b_sb = work.tile([P, PACK, P], F32, name="b_sb")
            src = st[c]["b"][:].rearrange("p (m t) -> p t m", t=PACK)
            if c == 1:
                nc.vector.tensor_copy(b_sb[:], src)
            else:
                nc.scalar.copy(out=b_sb[:], in_=src)
            st[c]["b_sb"] = b_sb

        def gap(c):
            z = work.tile([P, PACK, P], F32, name="z")
            nc.vector.tensor_tensor(z[:], st[c]["a"][:].rearrange("p (m t) -> p t m", t=PACK), st[c]["b_sb"][:], ALU.subtract)
            st[c]["z"] = z

        def squash(c):
            th = work.tile([P, PACK, P], F32, name="th")
            for ts in pieces(c):
                nc.scalar.activation(out=th[:, ts, :], in_=st[c]["z"][:, ts, :], func=ACT.Tanh)
            st[c]["th"] = th

        def turn(c, src, dst):
            bank = psum.tile([P, PACK, P], F32, name="bank", tag="bank")
            for t in range(PACK):
                nc.tensor.transpose(bank[:, t, :], st[c][src][:, t, :], ident[:])
            st[c][dst] = bank

        def weigh(c):
            d = work.tile([P, P, PACK], BF16, name="d", align_bytes=64)
            nc.vector.tensor_tensor(
                d[:], st[c]["th_t"][:].rearrange("p t j -> p j t"), us_sb[:].to_broadcast([P, P, PACK]), ALU.mult
            )
            st[c]["d"] = d

        def quantise_d(c):
            codes = work.tile([P, P], U32, name="d_codes", align_bytes=64)
            scales = work.tile([P, P], U8, name="d_scales", align_bytes=64)
            nc.vector.quantize_mx(out=codes[:].bitcast(E5M2), scales=scales[:], in_=st[c]["d"][:].rearrange("p j t -> p (j t)"))
            st[c]["dq"] = (codes, scales)

        def way_back(c):
            codes, scales = st[c]["dq"]
            bank = psum.tile([P, K], F32, name="bank", tag="bank")
            nc.tensor.matmul_mx(
                out=bank[:], lhsT=codes[:].bitcast(E5M2), lhsT_scale=scales[:],
                rhs=wt[:].bitcast(E4M3), rhs_scale=wts[:], start=True, stop=True,
            )
            st[c]["q"] = bank

        def scale_rows(c):
            y_t = work.tile([P, PACK, P], F32, name="y_t")
            src = st[c]["q"][:].rearrange("p (m t) -> p t m", t=PACK)
            for ts in pieces(c):
                nc.scalar.activation(out=y_t[:, ts, :], in_=src[:, ts, :], func=ACT.Copy, scale=rw_sb[:, c : c + 1])
            st[c]["y_t"] = y_t

        def copy(on_vector, out, src):
            if on_vector:
                nc.vector.tensor_copy(out, src)
            else:
                nc.scalar.copy(out=out, in_=src)

        def round_y(c, on_vector, src):
            y_bf = work.tile([P, P, PACK], BF16, name="y_bf", align_bytes=64)
            copy(on_vector, y_bf[:], src[:].rearrange("p t j -> p j t"))
            st[c]["y_bf"] = y_bf

        def store_y(c):
            y_sb = work.tile([P, PACK, P], F32, name="y_sb")
            early = c < 2
            if not early:
                round_y(c, c == CHUNKS - 1, st[c]["y"])
            copy(early, y_sb[:], st[c]["y"][:])
            nc.sync.dma_start(out=out_view[:, :, c * P : (c + 1) * P], in_=y_sb[:])
            if early:
                round_y(c, True, y_sb)

        def quantise_y(c):
            cols = slice(c * P, (c + 1) * P)
            nc.vector.quantize_mx(
                out=y_codes[:, cols].bitcast(E4M3), scales=y_scales[:, cols], in_=st[c]["y_bf"][:].rearrange("p j t -> p (j t)")
            )
            if c % 2 == 1:
                pair = slice((c - 1) * P, (c + 1) * P)
                nc.sync.dma_start(out=words_view[:, pair], in_=y_codes[:, pair].bitcast(I32))

        product(0, "b", wb, wbs, E2M1)
        for c in range(CHUNKS):
            if c + 1 < CHUNKS:
                product(c + 1, "b", wb, wbs, E2M1)
            product(c, "a", wa, was, E4M3)

        stages = [
            copy_b, gap, squash, lambda c: turn(c, "th", "th_t"), weigh, quantise_d, way_back,
            scale_rows, lambda c: turn(c, "y_t", "y"), store_y, quantise_y,
        ]
        for stage in stages:
            for c in range(CHUNKS):
                stage(c)

        scales_view = out_2[0].bitcast(I32)
        for q in range(4):
            both[q % 2].dma_start(out=scales_view[4 * q : 4 * q + 4, :], in_=y_scales[32 * q : 32 * q + 4, :].bitcast(I32))
